import numpy as np
import ml_dtypes

BF16 = ml_dtypes.bfloat16


def bf(x):
    return np.asarray(x, np.float32).astype(BF16)


def f32(x):
    return np.asarray(x, np.float32)


def f64(x):
    return np.asarray(x).astype(np.float64)


def striped(idx):
    return np.tile(idx.reshape(-1, 16).T, (8, 1))


S, K, M, N = 256, 128, 512, 192


def setup_inputs():
    return {"base": bf(np.random.standard_normal((M, S))), "x": bf(np.random.standard_normal((K, N))), "w": bf(np.random.standard_normal((K, M)) / np.sqrt(K)), "c": f32(0.2 + 0.8 * np.random.random_sample((1, S))), "offs": striped(np.random.permutation(S)[:N])}


def reference(base, x, w, c, offs):
    idx = offs[:16].T.reshape(-1)
    z = f64(base).copy()
    z[:, idx] = f64(w).T @ f64(x)
    return z * f64(c)

@@ -1,0 +1,53 @@
+import concourse.mybir as mybir
+from concourse.masks import make_identity
+
+BF16, F32, U16 = mybir.dt.bfloat16, mybir.dt.float32, mybir.dt.uint16
+
+P = 128
+M = 512
+S = 256
+N = 192
+BLOCKS = M // P
+
+FLOPS = 2 * P * M * N
+
+
+def tile_scatter_matmul_kernel(tc, base, x, w, c, offs, out):
+    nc = tc.nc
+    with (
+        tc.tile_pool(name="held", bufs=1) as held,
+        tc.psum_pool(name="psum", bufs=1) as psum,
+    ):
+        offsets = held.tile([P, N // 16], U16, name="offsets")
+        nc.sync.dma_start(offsets[:], offs)
+
+        base_sb = held.tile([P, BLOCKS, S], BF16, name="base_sb")
+        nc.sync.dma_start(base_sb[:], base.rearrange("(a p) s -> p a s", p=P))
+        w_sb = held.tile([P, M], BF16, name="w_sb")
+        nc.scalar.dma_start(w_sb[:], w)
+        x_sb = held.tile([P, N], BF16, name="x_sb")
+        nc.scalar.dma_start(x_sb[:], x)
+        c_sb = held.tile([P, S], F32, name="c_sb")
+        nc.gpsimd.dma_start(c_sb[:], c.partition_broadcast(P))
+
+        ident = held.tile([P, P], BF16, name="ident")
+        make_identity(nc, ident[:])
+
+        windows = [psum.tile([P, S], F32, name="window%d" % a) for a in range(BLOCKS)]
+        for a in range(BLOCKS):
+            nc.tensor.matmul(windows[a][:], ident[:], base_sb[:, a, :], start=True, stop=True)
+
+        for a in range(BLOCKS):
+            nc.tensor.matmul(
+                windows[a][:].indirect(offsets[:]),
+                w_sb[:, a * P : (a + 1) * P],
+                x_sb[:],
+                start=True,
+                stop=True,
+            )
+
+        for a in range(BLOCKS):
+            scaled = held.tile([P, S], F32, name="scaled%d" % a)
+            nc.vector.tensor_tensor(scaled[:], windows[a][:], c_sb[:], mybir.AluOpType.mult)
+            queue = nc.sync if a % 2 == 0 else nc.scalar
+            queue.dma_start(out[a * P : (a + 1) * P, :], scaled[:])

@@ -18,24 +18,25 @@ def tile_scatter_matmul_kernel(tc, base, x, w, c, offs, out):
         tc.tile_pool(name="held", bufs=1) as held,
         tc.psum_pool(name="psum", bufs=1) as psum,
     ):
-        offsets = held.tile([P, N // 16], U16, name="offsets")
-        nc.sync.dma_start(offsets[:], offs)
-
-        base_sb = held.tile([P, BLOCKS, S], BF16, name="base_sb")
-        nc.sync.dma_start(base_sb[:], base.rearrange("(a p) s -> p a s", p=P))
-        w_sb = held.tile([P, M], BF16, name="w_sb")
-        nc.scalar.dma_start(w_sb[:], w)
-        x_sb = held.tile([P, N], BF16, name="x_sb")
-        nc.scalar.dma_start(x_sb[:], x)
-        c_sb = held.tile([P, S], F32, name="c_sb")
-        nc.gpsimd.dma_start(c_sb[:], c.partition_broadcast(P))
-
         ident = held.tile([P, P], BF16, name="ident")
         make_identity(nc, ident[:])
 
+        base_sb = [held.tile([P, S], BF16, name="base%d" % a) for a in range(BLOCKS)]
+        for a in range(BLOCKS):
+            queue = nc.sync if a % 2 == 0 else nc.scalar
+            queue.dma_start(base_sb[a][:], base[a * P : (a + 1) * P, :])
+        offsets = held.tile([P, N // 16], U16, name="offsets")
+        nc.sync.dma_start(offsets[:], offs)
+        x_sb = held.tile([P, N], BF16, name="x_sb")
+        nc.sync.dma_start(x_sb[:], x)
+        w_sb = held.tile([P, M], BF16, name="w_sb")
+        nc.scalar.dma_start(w_sb[:], w)
+        c_sb = held.tile([P, S], F32, name="c_sb")
+        nc.scalar.dma_start(c_sb[:], c.partition_broadcast(P))
+
         windows = [psum.tile([P, S], F32, name="window%d" % a) for a in range(BLOCKS)]
         for a in range(BLOCKS):
-            nc.tensor.matmul(windows[a][:], ident[:], base_sb[:, a, :], start=True, stop=True)
+            nc.tensor.matmul(windows[a][:], ident[:], base_sb[a][:], start=True, stop=True)
 
         for a in range(BLOCKS):
             nc.tensor.matmul(

@@ -20,6 +20,8 @@ def tile_scatter_matmul_kernel(tc, base, x, w, c, offs, out):
     ):
         ident = held.tile([P, P], BF16, name="ident")
         make_identity(nc, ident[:])
+        c_sb = held.tile([P, S], F32, name="c_sb")
+        nc.gpsimd.dma_start(c_sb[:], c.partition_broadcast(P))
 
         base_sb = [held.tile([P, S], BF16, name="base%d" % a) for a in range(BLOCKS)]
         for a in range(BLOCKS):
@@ -31,8 +33,6 @@ def tile_scatter_matmul_kernel(tc, base, x, w, c, offs, out):
         nc.sync.dma_start(x_sb[:], x)
         w_sb = held.tile([P, M], BF16, name="w_sb")
         nc.scalar.dma_start(w_sb[:], w)
-        c_sb = held.tile([P, S], F32, name="c_sb")
-        nc.scalar.dma_start(c_sb[:], c.partition_broadcast(P))
 
         windows = [psum.tile([P, S], F32, name="window%d" % a) for a in range(BLOCKS)]
         for a in range(BLOCKS):

@@ -18,25 +18,31 @@ def tile_scatter_matmul_kernel(tc, base, x, w, c, offs, out):
         tc.tile_pool(name="held", bufs=1) as held,
         tc.psum_pool(name="psum", bufs=1) as psum,
     ):
-        ident = held.tile([P, P], BF16, name="ident")
-        make_identity(nc, ident[:])
-        c_sb = held.tile([P, S], F32, name="c_sb")
-        nc.gpsimd.dma_start(c_sb[:], c.partition_broadcast(P))
-
-        base_sb = [held.tile([P, S], BF16, name="base%d" % a) for a in range(BLOCKS)]
-        for a in range(BLOCKS):
-            queue = nc.sync if a % 2 == 0 else nc.scalar
-            queue.dma_start(base_sb[a][:], base[a * P : (a + 1) * P, :])
         offsets = held.tile([P, N // 16], U16, name="offsets")
         nc.sync.dma_start(offsets[:], offs)
-        x_sb = held.tile([P, N], BF16, name="x_sb")
-        nc.sync.dma_start(x_sb[:], x)
+
+        base_sb = held.tile([P, BLOCKS, S], BF16, name="base_sb")
+        nc.sync.dma_start(base_sb[:], base.rearrange("(a p) s -> p a s", p=P))
+        c_row = held.tile([1, S], F32, name="c_row")
+        nc.scalar.dma_start(c_row[:], c)
+        ones_row = held.tile([1, P], F32, name="ones_row")
+        nc.vector.memset(ones_row[:], 1.0)
+        c_psum = psum.tile([P, S], F32, name="c_psum")
+        nc.tensor.matmul(c_psum[:], ones_row[:], c_row[:], start=True, stop=True)
+        c_sb = held.tile([P, S], F32, name="c_sb")
+        nc.vector.tensor_copy(c_sb[:], c_psum[:])
+
         w_sb = held.tile([P, M], BF16, name="w_sb")
         nc.scalar.dma_start(w_sb[:], w)
+        x_sb = held.tile([P, N], BF16, name="x_sb")
+        nc.scalar.dma_start(x_sb[:], x)
+
+        ident = held.tile([P, P], BF16, name="ident")
+        make_identity(nc, ident[:])
 
         windows = [psum.tile([P, S], F32, name="window%d" % a) for a in range(BLOCKS)]
         for a in range(BLOCKS):
-            nc.tensor.matmul(windows[a][:], ident[:], base_sb[a][:], start=True, stop=True)
+            nc.tensor.matmul(windows[a][:], ident[:], base_sb[:, a, :], start=True, stop=True)
 
         for a in range(BLOCKS):
             nc.tensor.matmul(

@@ -9,6 +9,9 @@ S = 256
 N = 192
 BLOCKS = M // P
 
+WARM_COLUMNS = 512
+WARM_MATMULS = 2
+
 FLOPS = 2 * P * M * N
 
 
@@ -18,31 +21,39 @@ def tile_scatter_matmul_kernel(tc, base, x, w, c, offs, out):
         tc.tile_pool(name="held", bufs=1) as held,
         tc.psum_pool(name="psum", bufs=1) as psum,
     ):
+        c_padded = held.tile([P, S], F32, name="c_padded")
+        nc.gpsimd.memset(c_padded[:], 0.0)
+        nc.scalar.dma_start(c_padded[0:1, :], c)
+
+        base_sb = [held.tile([P, S], BF16, name="base%d" % a) for a in range(BLOCKS)]
+        for a in range(BLOCKS):
+            queue = nc.sync if a % 2 == 0 else nc.scalar
+            queue.dma_start(base_sb[a][:], base[a * P : (a + 1) * P, :])
         offsets = held.tile([P, N // 16], U16, name="offsets")
         nc.sync.dma_start(offsets[:], offs)
-
-        base_sb = held.tile([P, BLOCKS, S], BF16, name="base_sb")
-        nc.sync.dma_start(base_sb[:], base.rearrange("(a p) s -> p a s", p=P))
-        c_row = held.tile([1, S], F32, name="c_row")
-        nc.scalar.dma_start(c_row[:], c)
-        ones_row = held.tile([1, P], F32, name="ones_row")
-        nc.vector.memset(ones_row[:], 1.0)
-        c_psum = psum.tile([P, S], F32, name="c_psum")
-        nc.tensor.matmul(c_psum[:], ones_row[:], c_row[:], start=True, stop=True)
-        c_sb = held.tile([P, S], F32, name="c_sb")
-        nc.vector.tensor_copy(c_sb[:], c_psum[:])
-
         w_sb = held.tile([P, M], BF16, name="w_sb")
-        nc.scalar.dma_start(w_sb[:], w)
+        nc.sync.dma_start(w_sb[:], w)
         x_sb = held.tile([P, N], BF16, name="x_sb")
         nc.scalar.dma_start(x_sb[:], x)
 
+        zeros = held.tile([P, WARM_COLUMNS], BF16, name="zeros")
+        nc.vector.memset(zeros[:], 0.0)
+        unread = psum.tile([P, WARM_COLUMNS], F32, name="unread")
+        for i in range(WARM_MATMULS):
+            nc.tensor.matmul(unread[:], zeros[:, 0:P], zeros[:], start=True, stop=True)
+
+        ones = held.tile([P, P], F32, name="ones")
+        nc.vector.memset(ones[:], 1.0)
+        c_psum = psum.tile([P, S], F32, name="c_psum")
+        nc.tensor.matmul(c_psum[:], ones[:], c_padded[:], start=True, stop=True)
+        c_sb = held.tile([P, S], F32, name="c_sb")
+        nc.vector.tensor_copy(c_sb[:], c_psum[:])
+
         ident = held.tile([P, P], BF16, name="ident")
         make_identity(nc, ident[:])
-
         windows = [psum.tile([P, S], F32, name="window%d" % a) for a in range(BLOCKS)]
         for a in range(BLOCKS):
-            nc.tensor.matmul(windows[a][:], ident[:], base_sb[:, a, :], start=True, stop=True)
+            nc.tensor.matmul(windows[a][:], ident[:], base_sb[a][:], start=True, stop=True)
 
         for a in range(BLOCKS):
             nc.tensor.matmul(

@@ -22,8 +22,8 @@ def tile_scatter_matmul_kernel(tc, base, x, w, c, offs, out):
         tc.psum_pool(name="psum", bufs=1) as psum,
     ):
         c_padded = held.tile([P, S], F32, name="c_padded")
-        nc.gpsimd.memset(c_padded[:], 0.0)
-        nc.scalar.dma_start(c_padded[0:1, :], c)
+        nc.gpsimd.memset(c_padded[0 : P - 1, :], 0.0)
+        nc.scalar.dma_start(c_padded[P - 1 : P, :], c)
 
         base_sb = [held.tile([P, S], BF16, name="base%d" % a) for a in range(BLOCKS)]
         for a in range(BLOCKS):

@@ -9,8 +9,8 @@ S = 256
 N = 192
 BLOCKS = M // P
 
-WARM_COLUMNS = 512
-WARM_MATMULS = 2
+WARM_COLUMNS = P
+WARM_MATMULS = 8
 
 FLOPS = 2 * P * M * N
 
@@ -21,6 +21,9 @@ def tile_scatter_matmul_kernel(tc, base, x, w, c, offs, out):
         tc.tile_pool(name="held", bufs=1) as held,
         tc.psum_pool(name="psum", bufs=1) as psum,
     ):
+        zeros = held.tile([P, WARM_COLUMNS], BF16, name="zeros")
+        nc.gpsimd.memset(zeros[:], 0.0)
+
         c_padded = held.tile([P, S], F32, name="c_padded")
         nc.gpsimd.memset(c_padded[0 : P - 1, :], 0.0)
         nc.scalar.dma_start(c_padded[P - 1 : P, :], c)
@@ -36,11 +39,9 @@ def tile_scatter_matmul_kernel(tc, base, x, w, c, offs, out):
         x_sb = held.tile([P, N], BF16, name="x_sb")
         nc.scalar.dma_start(x_sb[:], x)
 
-        zeros = held.tile([P, WARM_COLUMNS], BF16, name="zeros")
-        nc.vector.memset(zeros[:], 0.0)
         unread = psum.tile([P, WARM_COLUMNS], F32, name="unread")
         for i in range(WARM_MATMULS):
-            nc.tensor.matmul(unread[:], zeros[:, 0:P], zeros[:], start=True, stop=True)
+            nc.tensor.matmul(unread[:], zeros[:], zeros[:], start=True, stop=True)
 
         ones = held.tile([P, P], F32, name="ones")
         nc.vector.memset(ones[:], 1.0)

@@ -26,7 +26,7 @@ def tile_scatter_matmul_kernel(tc, base, x, w, c, offs, out):
 
         c_padded = held.tile([P, S], F32, name="c_padded")
         nc.gpsimd.memset(c_padded[0 : P - 1, :], 0.0)
-        nc.scalar.dma_start(c_padded[P - 1 : P, :], c)
+        nc.sync.dma_start(c_padded[P - 1 : P, :], c)
 
         base_sb = [held.tile([P, S], BF16, name="base%d" % a) for a in range(BLOCKS)]
         for a in range(BLOCKS):
@@ -34,10 +34,10 @@ def tile_scatter_matmul_kernel(tc, base, x, w, c, offs, out):
             queue.dma_start(base_sb[a][:], base[a * P : (a + 1) * P, :])
         offsets = held.tile([P, N // 16], U16, name="offsets")
         nc.sync.dma_start(offsets[:], offs)
-        w_sb = held.tile([P, M], BF16, name="w_sb")
-        nc.sync.dma_start(w_sb[:], w)
         x_sb = held.tile([P, N], BF16, name="x_sb")
-        nc.scalar.dma_start(x_sb[:], x)
+        nc.sync.dma_start(x_sb[:], x)
+        w_sb = held.tile([P, M], BF16, name="w_sb")
+        nc.scalar.dma_start(w_sb[:], w)
 
         unread = psum.tile([P, WARM_COLUMNS], F32, name="unread")
         for i in range(WARM_MATMULS):

@@ -21,7 +21,7 @@ def tile_scatter_matmul_kernel(tc, base, x, w, c, offs, out):
         tc.tile_pool(name="held", bufs=1) as held,
         tc.psum_pool(name="psum", bufs=1) as psum,
     ):
-        zeros = held.tile([P, WARM_COLUMNS], BF16, name="zeros")
+        zeros = held.tile([P, 1], BF16, name="zeros")
         nc.gpsimd.memset(zeros[:], 0.0)
 
         c_padded = held.tile([P, S], F32, name="c_padded")
@@ -41,7 +41,13 @@ def tile_scatter_matmul_kernel(tc, base, x, w, c, offs, out):
 
         unread = psum.tile([P, WARM_COLUMNS], F32, name="unread")
         for i in range(WARM_MATMULS):
-            nc.tensor.matmul(unread[:], zeros[:], zeros[:], start=True, stop=True)
+            nc.tensor.matmul(
+                unread[:],
+                zeros[:].to_broadcast([P, P]),
+                zeros[:].to_broadcast([P, WARM_COLUMNS]),
+                start=True,
+                stop=True,
+            )
 
         ones = held.tile([P, P], F32, name="ones")
         nc.vector.memset(ones[:], 1.0)

@@ -74,5 +74,4 @@ def tile_scatter_matmul_kernel(tc, base, x, w, c, offs, out):
         for a in range(BLOCKS):
             scaled = held.tile([P, S], F32, name="scaled%d" % a)
             nc.vector.tensor_tensor(scaled[:], windows[a][:], c_sb[:], mybir.AluOpType.mult)
-            queue = nc.sync if a % 2 == 0 else nc.scalar
-            queue.dma_start(out[a * P : (a + 1) * P, :], scaled[:])
+            nc.sync.dma_start(out[a * P : (a + 1) * P, :], scaled[:])

import concourse.mybir as mybir
from concourse.masks import make_identity

BF16, F32, U16 = mybir.dt.bfloat16, mybir.dt.float32, mybir.dt.uint16

P = 128
M = 512
S = 256
N = 192
BLOCKS = M // P

WARM_COLUMNS = P
WARM_MATMULS = 8

FLOPS = 2 * P * M * N


def tile_scatter_matmul_kernel(tc, base, x, w, c, offs, out):
    nc = tc.nc
    with (
        tc.tile_pool(name="held", bufs=1) as held,
        tc.psum_pool(name="psum", bufs=1) as psum,
    ):
        zeros = held.tile([P, 1], BF16, name="zeros")
        nc.gpsimd.memset(zeros[:], 0.0)

        c_padded = held.tile([P, S], F32, name="c_padded")
        nc.gpsimd.memset(c_padded[0 : P - 1, :], 0.0)
        nc.sync.dma_start(c_padded[P - 1 : P, :], c)

        base_sb = [held.tile([P, S], BF16, name="base%d" % a) for a in range(BLOCKS)]
        for a in range(BLOCKS):
            queue = nc.sync if a % 2 == 0 else nc.scalar
            queue.dma_start(base_sb[a][:], base[a * P : (a + 1) * P, :])
        offsets = held.tile([P, N // 16], U16, name="offsets")
        nc.sync.dma_start(offsets[:], offs)
        x_sb = held.tile([P, N], BF16, name="x_sb")
        nc.sync.dma_start(x_sb[:], x)
        w_sb = held.tile([P, M], BF16, name="w_sb")
        nc.scalar.dma_start(w_sb[:], w)

        unread = psum.tile([P, WARM_COLUMNS], F32, name="unread")
        for i in range(WARM_MATMULS):
            nc.tensor.matmul(
                unread[:],
                zeros[:].to_broadcast([P, P]),
                zeros[:].to_broadcast([P, WARM_COLUMNS]),
                start=True,
                stop=True,
            )

        ones = held.tile([P, P], F32, name="ones")
        nc.vector.memset(ones[:], 1.0)
        c_psum = psum.tile([P, S], F32, name="c_psum")
        nc.tensor.matmul(c_psum[:], ones[:], c_padded[:], start=True, stop=True)
        c_sb = held.tile([P, S], F32, name="c_sb")
        nc.vector.tensor_copy(c_sb[:], c_psum[:])

        ident = held.tile([P, P], BF16, name="ident")
        make_identity(nc, ident[:])
        windows = [psum.tile([P, S], F32, name="window%d" % a) for a in range(BLOCKS)]
        for a in range(BLOCKS):
            nc.tensor.matmul(windows[a][:], ident[:], base_sb[a][:], start=True, stop=True)

        for a in range(BLOCKS):
            nc.tensor.matmul(
                windows[a][:].indirect(offsets[:]),
                w_sb[:, a * P : (a + 1) * P],
                x_sb[:],
                start=True,
                stop=True,
            )

        for a in range(BLOCKS):
            scaled = held.tile([P, S], F32, name="scaled%d" % a)
            nc.vector.tensor_tensor(scaled[:], windows[a][:], c_sb[:], mybir.AluOpType.mult)
            nc.sync.dma_start(out[a * P : (a + 1) * P, :], scaled[:])
